import numpy as np, ml_dtypes
CORES = [45,53,77,117,47,55,79,119]
N = 8
F = 512
def setup_inputs(rng):
    return {"a": rng.standard_normal((N, 128, 128), dtype=np.float32).astype(ml_dtypes.bfloat16), "b": rng.standard_normal((N, 128, F), dtype=np.float32).astype(ml_dtypes.bfloat16)}
def setup_inputs_big(rng):
    d = setup_inputs(rng)
    for k in ("a", "b"): d[k] = (d[k].astype(np.float32) * 1024.0).astype(d[k].dtype)
    return d
def setup_inputs_small(rng):
    d = setup_inputs(rng)
    for k in ("a", "b"): d[k] = (d[k].astype(np.float32) * (1 / 1024.0)).astype(d[k].dtype)
    return d
def setup_inputs_apart(rng):
    d = setup_inputs(rng)
    f = (10.0 ** rng.permutation(np.linspace(-1.5, 1.5, N))).astype(np.float32).reshape(N, 1, 1)
    for k in ("a", "b"): d[k] = (d[k].astype(np.float32) * f).astype(d[k].dtype)
    return d
def reference(a, b):
    s = (a.astype(np.float64).sum(axis=0).T @ b.astype(np.float64).sum(axis=0)).astype(ml_dtypes.bfloat16 if a.dtype != np.float64 else np.float64)
    return {"y": np.broadcast_to(s, (N,) + s.shape)}

@@ -1,0 +1,132 @@
+from concourse.bass import DstId, RemoteDMATransfer
+from concourse.mybir import AluOpType
+
+KA = 128
+F = 512
+W = KA + F
+H = F // 2
+
+SCRATCH = {
+    "x": ("sbuf", [128, W], "bfloat16"),
+    "lp": ("sbuf", [128, W], "bfloat16"),
+    "lr0": ("sbuf", [128, W], "bfloat16"),
+    "lr1": ("sbuf", [128, W], "bfloat16"),
+    "so": ("sbuf", [128, W], "bfloat16"),
+    "se": ("sbuf", [128, W], "bfloat16"),
+    "asum": ("sbuf", [128, KA], "bfloat16"),
+    "yo": ("sbuf", [128, F], "bfloat16"),
+    "ta": ("psum", [128, 512], "float32"),
+    "tb": ("psum", [128, 512], "float32"),
+    "y0": ("psum", [128, 512], "float32"),
+    "y1": ("psum", [128, 512], "float32"),
+}
+SEMAPHORES = ["ld", "st", "snt", "arrp", "arrr", "arro", "arre",
+              "sa", "sb", "vo", "va", "tm0", "tm1", "vc"]
+
+
+def _bits(mask):
+    return bin(mask).count("1")
+
+
+def _plan(core, T, topo):
+    cores = list(T.cores)
+    chip = topo.chip(core)
+    chips = sorted({topo.chip(c) for c in cores})
+    on = {ch: [c for c in cores if topo.chip(c) == ch] for ch in chips}
+    folder = {ch: [c for c in on[ch] if all(topo.may_write(c, d) for d in cores if d != c)][0] for ch in chips}
+    mine = sorted([chip] + [ch for ch in chips if topo.same_plane(chip, ch)])
+    other = [ch for ch in chips if ch not in mine]
+    plane_partner = [ch for ch in mine if ch != chip][0]
+    across = other[mine.index(chip)]
+    return {
+        "folder": folder[chip],
+        "leaf": [c for c in on[chip] if c != folder[chip]][0],
+        "far_folder": folder[plane_partner],
+        "across": on[across],
+    }
+
+
+def rank_program(g, core, T, topo):
+    if T.rank_of(core) is None:
+        return
+    p = _plan(core, T, topo)
+    s = T.sem
+    add = AluOpType.add
+    is_folder = core == p["folder"]
+    chipmate = p["leaf"] if is_folder else p["folder"]
+    m_off = topo.mask(core, p["far_folder"])
+    m_on = topo.mask(core, chipmate) & ~m_off
+    n_off, n_on = _bits(m_off), _bits(m_on)
+
+    def dst(c):
+        rid, pid, _ = topo.addr(c)
+        return DstId(rid=rid, pnc=pid)
+
+    def send(out_ap, to, sem, mask):
+        rid, pid, _ = topo.addr(to)
+        g.remote_dma(out_ap=out_ap, in_ap=T.x[:], remote_sem=sem, local_sem=s.snt, pid=pid, routing_id=rid,
+                     dma_engine_mask=mask)
+
+    xa, xb = slice(0, KA), slice(KA, W)
+    h0, h1 = slice(KA, KA + H), slice(KA + H, W)
+
+    g.sync.dma_start(T.x[:, xa], T.a[:]).then_inc(s.ld, 16)
+    g.scalar.dma_start(T.x[:, xb], T.b[:]).then_inc(s.ld, 16)
+    g.wait_ge(s.ld, 32)
+
+    v, t = g.vector, g.tensor
+    if not is_folder:
+        send(T.lr0[:], p["far_folder"], s.arrr, m_off)
+        send(T.lp[:], p["folder"], s.arrp, m_on)
+        sent = n_off + n_on
+        t.wait_ge(s.arro, n_on)
+        v.wait_ge(s.arro, n_on)
+    else:
+        send(T.lr1[:], p["far_folder"], s.arrr, m_off)
+        g.wait_ge(s.arrp, n_on)
+        g.wait_ge(s.arrr, 2 * n_off)
+        four = [T.x[:], T.lp[:], T.lr0[:], T.lr1[:]]
+        g.remote_dma_fused([RemoteDMATransfer(dst_ids=[dst(c) for c in p["across"]], dma_engine_mask=m_off,
+                                              remote_sem=s.arre, srcs=four, dsts=[T.se[:] for _ in p["across"]],
+                                              alu_op=1)], local_sem=s.snt)
+        g.remote_dma_fused([RemoteDMATransfer(dst_ids=[dst(p["leaf"])], dma_engine_mask=m_on,
+                                              remote_sem=s.arro, srcs=four, dsts=[T.so[:]],
+                                              alu_op=1)], local_sem=s.snt)
+        sent = n_off + n_off + n_on
+        v.wait_ge(s.ld, 32)
+        v.wait_ge(s.arrp, n_on)
+        v.tensor_tensor(T.ta[:, 0:KA], T.x[:, xa], T.lp[:, xa], add).then_inc(s.sa, 1)
+        v.tensor_tensor(T.tb[:, 0:F], T.x[:, xb], T.lp[:, xb], add).then_inc(s.sb, 1)
+        v.wait_ge(s.arrr, 2 * n_off)
+        v.wait_ge(s.sa, 1)
+        v.tensor_tensor(T.ta[:, 0:KA], T.ta[:, 0:KA], T.lr0[:, xa], add).then_inc(s.sa, 1)
+        v.wait_ge(s.sb, 1)
+        v.tensor_tensor(T.tb[:, 0:F], T.tb[:, 0:F], T.lr0[:, xb], add).then_inc(s.sb, 1)
+        v.wait_ge(s.sa, 2)
+        v.tensor_tensor(T.so[:, xa], T.ta[:, 0:KA], T.lr1[:, xa], add).then_inc(s.vo, 1)
+        v.wait_ge(s.sb, 2)
+        v.tensor_tensor(T.so[:, xb], T.tb[:, 0:F], T.lr1[:, xb], add).then_inc(s.vo, 1)
+        t.wait_ge(s.vo, 2)
+        v.wait_ge(s.vo, 2)
+
+    t.matmul(T.y0[:, 0:H], T.so[:, xa], T.so[:, h0], True, False)
+    t.matmul(T.y1[:, 0:H], T.so[:, xa], T.so[:, h1], True, False)
+    t.wait_ge(s.arre, n_off)
+    t.matmul(T.y0[:, 0:H], T.se[:, xa], T.so[:, h0], False, False)
+    t.matmul(T.y1[:, 0:H], T.se[:, xa], T.so[:, h1], False, False)
+    t.wait_ge(s.va, 1)
+    t.matmul(T.y0[:, 0:H], T.asum[:], T.se[:, h0], False, True).then_inc(s.tm0, 1)
+    t.matmul(T.y1[:, 0:H], T.asum[:], T.se[:, h1], False, True).then_inc(s.tm1, 1)
+
+    v.wait_ge(s.arre, n_off)
+    v.tensor_tensor(T.asum[:], T.so[:, xa], T.se[:, xa], add).then_inc(s.va, 1)
+    v.wait_ge(s.tm0, 1)
+    v.tensor_copy(T.yo[:, 0:H], T.y0[:, 0:H]).then_inc(s.vc, 1)
+    v.wait_ge(s.tm1, 1)
+    v.tensor_copy(T.yo[:, H:F], T.y1[:, 0:H]).then_inc(s.vc, 1)
+
+    g.sync.wait_ge(s.vc, 2)
+    g.sync.dma_start(T.y[:], T.yo[:]).then_inc(s.st, 16)
+
+    g.wait_ge(s.snt, sent)
+    g.wait_ge(s.st, 16)

@@ -5,10 +5,13 @@ KA = 128
 F = 512
 W = KA + F
 H = F // 2
+K = 4
+PW = W // K
 
 SCRATCH = {
     "x": ("sbuf", [128, W], "bfloat16"),
-    "lp": ("sbuf", [128, W], "bfloat16"),
+    "lc0": ("sbuf", [128, W], "bfloat16"),
+    "lc1": ("sbuf", [128, W], "bfloat16"),
     "lr0": ("sbuf", [128, W], "bfloat16"),
     "lr1": ("sbuf", [128, W], "bfloat16"),
     "so": ("sbuf", [128, W], "bfloat16"),
@@ -16,117 +19,135 @@ SCRATCH = {
     "asum": ("sbuf", [128, KA], "bfloat16"),
     "yo": ("sbuf", [128, F], "bfloat16"),
     "ta": ("psum", [128, 512], "float32"),
-    "tb": ("psum", [128, 512], "float32"),
     "y0": ("psum", [128, 512], "float32"),
     "y1": ("psum", [128, 512], "float32"),
 }
-SEMAPHORES = ["ld", "st", "snt", "arrp", "arrr", "arro", "arre",
-              "sa", "sb", "vo", "va", "tm0", "tm1", "vc"]
+SEMAPHORES = ["ld", "st", "snt", "arrc", "arrr", "arro", "arre", "sa", "vo", "va", "tm0", "tm1", "vc"]
 
 
 def _bits(mask):
     return bin(mask).count("1")
 
 
+def _groups(mask, k):
+    b = [1 << i for i in range(mask.bit_length()) if mask >> i & 1]
+    n = len(b) // k
+    return [sum(b[i * n:(i + 1) * n]) for i in range(k)]
+
+
 def _plan(core, T, topo):
     cores = list(T.cores)
     chip = topo.chip(core)
     chips = sorted({topo.chip(c) for c in cores})
-    on = {ch: [c for c in cores if topo.chip(c) == ch] for ch in chips}
-    folder = {ch: [c for c in on[ch] if all(topo.may_write(c, d) for d in cores if d != c)][0] for ch in chips}
+    if chip not in chips:
+        return None
+    every = range(topo.CHIPS * topo.CORES_PER_CHIP)
+
+    def ranks(ch):
+        return [c for c in cores if topo.chip(c) == ch]
+
+    def folders(ch):
+        able = [c for c in every if topo.chip(c) == ch and all(topo.may_write(c, d) for d in cores if d != c)]
+        return ([c for c in able if c in cores] + [c for c in able if c not in cores])[:K]
+
     mine = sorted([chip] + [ch for ch in chips if topo.same_plane(chip, ch)])
     other = [ch for ch in chips if ch not in mine]
-    plane_partner = [ch for ch in mine if ch != chip][0]
-    across = other[mine.index(chip)]
+    partner = [ch for ch in mine if ch != chip][0]
     return {
-        "folder": folder[chip],
-        "leaf": [c for c in on[chip] if c != folder[chip]][0],
-        "far_folder": folder[plane_partner],
-        "across": on[across],
+        "ranks": ranks(chip),
+        "folders": folders(chip),
+        "far_folders": folders(partner),
+        "across": ranks(other[mine.index(chip)]),
     }
 
 
 def rank_program(g, core, T, topo):
-    if T.rank_of(core) is None:
-        return
     p = _plan(core, T, topo)
+    if p is None or (core not in p["ranks"] and core not in p["folders"]):
+        return
     s = T.sem
     add = AluOpType.add
-    is_folder = core == p["folder"]
-    chipmate = p["leaf"] if is_folder else p["folder"]
-    m_off = topo.mask(core, p["far_folder"])
-    m_on = topo.mask(core, chipmate) & ~m_off
+    is_rank = core in p["ranks"]
+    is_folder = core in p["folders"]
+    m_off = topo.mask(core, p["far_folders"][0])
+    m_on = topo.mask(core, [c for c in p["ranks"] + p["folders"] if c != core][0]) & ~m_off
     n_off, n_on = _bits(m_off), _bits(m_on)
+    g_off, g_on = _groups(m_off, K), _groups(m_on, K)
+    cs = [slice(i * PW, (i + 1) * PW) for i in range(K)]
+    v, t = g.vector, g.tensor
+    sent = 0
 
     def dst(c):
         rid, pid, _ = topo.addr(c)
         return DstId(rid=rid, pnc=pid)
 
-    def send(out_ap, to, sem, mask):
-        rid, pid, _ = topo.addr(to)
-        g.remote_dma(out_ap=out_ap, in_ap=T.x[:], remote_sem=sem, local_sem=s.snt, pid=pid, routing_id=rid,
-                     dma_engine_mask=mask)
+    if is_rank:
+        g.sync.dma_start(T.x[:, 0:KA], T.a[:]).then_inc(s.ld, 16)
+        g.scalar.dma_start(T.x[:, KA:W], T.b[:]).then_inc(s.ld, 16)
+        g.wait_ge(s.ld, 32)
+        me = p["ranks"].index(core)
+        far, near = (T.lr0, T.lr1)[me], (T.lc0, T.lc1)[me]
+        g.remote_dma_fused([RemoteDMATransfer(dst_ids=[dst(f)], dma_engine_mask=g_off[i], remote_sem=s.arrr,
+                                              src=T.x[:, cs[i]], dst=far[:, cs[i]])
+                            for i, f in enumerate(p["far_folders"])], local_sem=s.snt)
+        g.remote_dma_fused([RemoteDMATransfer(dst_ids=[dst(f)], dma_engine_mask=g_on[i], remote_sem=s.arrc,
+                                              src=T.x[:, cs[i]], dst=near[:, cs[i]])
+                            for i, f in enumerate(p["folders"]) if f != core], local_sem=s.snt)
+        sent += n_off + sum(_bits(g_on[i]) for i, f in enumerate(p["folders"]) if f != core)
 
-    xa, xb = slice(0, KA), slice(KA, W)
-    h0, h1 = slice(KA, KA + H), slice(KA + H, W)
+    if is_folder:
+        j = p["folders"].index(core)
+        c = cs[j]
+        n_c = _bits(g_on[j]) * len([r for r in p["ranks"] if r != core])
+        n_r = _bits(g_off[j]) * len(p["ranks"])
+        here = [T.x if r == core else (T.lc0, T.lc1)[i] for i, r in enumerate(p["ranks"])]
+        four = here + [T.lr0, T.lr1]
+        home = [r for r in p["ranks"] if r != core]
+        g.wait_ge(s.arrc, n_c)
+        g.wait_ge(s.arrr, n_r)
+        g.remote_dma_fused([RemoteDMATransfer(dst_ids=[dst(r) for r in p["across"]], dma_engine_mask=m_off,
+                                              remote_sem=s.arre, srcs=[q[:, c] for q in four],
+                                              dsts=[T.se[:, c] for _ in p["across"]], alu_op=1),
+                            RemoteDMATransfer(dst_ids=[dst(r) for r in home], dma_engine_mask=m_on,
+                                              remote_sem=s.arro, srcs=[q[:, c] for q in four],
+                                              dsts=[T.so[:, c] for _ in home], alu_op=1)], local_sem=s.snt)
+        sent += n_off + n_on
+        if is_rank:
+            v.wait_ge(s.ld, 32)
+            v.wait_ge(s.arrc, n_c)
+            v.tensor_tensor(T.ta[:, 0:PW], four[0][:, c], four[1][:, c], add).then_inc(s.sa, 1)
+            v.wait_ge(s.arrr, n_r)
+            v.wait_ge(s.sa, 1)
+            v.tensor_tensor(T.ta[:, 0:PW], T.ta[:, 0:PW], four[2][:, c], add).then_inc(s.sa, 1)
+            v.wait_ge(s.sa, 2)
+            v.tensor_tensor(T.so[:, c], T.ta[:, 0:PW], four[3][:, c], add).then_inc(s.vo, 1)
+            v.wait_ge(s.vo, 1)
+            t.wait_ge(s.vo, 1)
 
-    g.sync.dma_start(T.x[:, xa], T.a[:]).then_inc(s.ld, 16)
-    g.scalar.dma_start(T.x[:, xb], T.b[:]).then_inc(s.ld, 16)
-    g.wait_ge(s.ld, 32)
-
-    v, t = g.vector, g.tensor
-    if not is_folder:
-        send(T.lr0[:], p["far_folder"], s.arrr, m_off)
-        send(T.lp[:], p["folder"], s.arrp, m_on)
-        sent = n_off + n_on
-        t.wait_ge(s.arro, n_on)
-        v.wait_ge(s.arro, n_on)
-    else:
-        send(T.lr1[:], p["far_folder"], s.arrr, m_off)
-        g.wait_ge(s.arrp, n_on)
-        g.wait_ge(s.arrr, 2 * n_off)
-        four = [T.x[:], T.lp[:], T.lr0[:], T.lr1[:]]
-        g.remote_dma_fused([RemoteDMATransfer(dst_ids=[dst(c) for c in p["across"]], dma_engine_mask=m_off,
-                                              remote_sem=s.arre, srcs=four, dsts=[T.se[:] for _ in p["across"]],
-                                              alu_op=1)], local_sem=s.snt)
-        g.remote_dma_fused([RemoteDMATransfer(dst_ids=[dst(p["leaf"])], dma_engine_mask=m_on,
-                                              remote_sem=s.arro, srcs=four, dsts=[T.so[:]],
-                                              alu_op=1)], local_sem=s.snt)
-        sent = n_off + n_off + n_on
-        v.wait_ge(s.ld, 32)
-        v.wait_ge(s.arrp, n_on)
-        v.tensor_tensor(T.ta[:, 0:KA], T.x[:, xa], T.lp[:, xa], add).then_inc(s.sa, 1)
-        v.tensor_tensor(T.tb[:, 0:F], T.x[:, xb], T.lp[:, xb], add).then_inc(s.sb, 1)
-        v.wait_ge(s.arrr, 2 * n_off)
-        v.wait_ge(s.sa, 1)
-        v.tensor_tensor(T.ta[:, 0:KA], T.ta[:, 0:KA], T.lr0[:, xa], add).then_inc(s.sa, 1)
-        v.wait_ge(s.sb, 1)
-        v.tensor_tensor(T.tb[:, 0:F], T.tb[:, 0:F], T.lr0[:, xb], add).then_inc(s.sb, 1)
-        v.wait_ge(s.sa, 2)
-        v.tensor_tensor(T.so[:, xa], T.ta[:, 0:KA], T.lr1[:, xa], add).then_inc(s.vo, 1)
-        v.wait_ge(s.sb, 2)
-        v.tensor_tensor(T.so[:, xb], T.tb[:, 0:F], T.lr1[:, xb], add).then_inc(s.vo, 1)
-        t.wait_ge(s.vo, 2)
-        v.wait_ge(s.vo, 2)
-
-    t.matmul(T.y0[:, 0:H], T.so[:, xa], T.so[:, h0], True, False)
-    t.matmul(T.y1[:, 0:H], T.so[:, xa], T.so[:, h1], True, False)
-    t.wait_ge(s.arre, n_off)
-    t.matmul(T.y0[:, 0:H], T.se[:, xa], T.so[:, h0], False, False)
-    t.matmul(T.y1[:, 0:H], T.se[:, xa], T.so[:, h1], False, False)
-    t.wait_ge(s.va, 1)
-    t.matmul(T.y0[:, 0:H], T.asum[:], T.se[:, h0], False, True).then_inc(s.tm0, 1)
-    t.matmul(T.y1[:, 0:H], T.asum[:], T.se[:, h1], False, True).then_inc(s.tm1, 1)
-
-    v.wait_ge(s.arre, n_off)
-    v.tensor_tensor(T.asum[:], T.so[:, xa], T.se[:, xa], add).then_inc(s.va, 1)
-    v.wait_ge(s.tm0, 1)
-    v.tensor_copy(T.yo[:, 0:H], T.y0[:, 0:H]).then_inc(s.vc, 1)
-    v.wait_ge(s.tm1, 1)
-    v.tensor_copy(T.yo[:, H:F], T.y1[:, 0:H]).then_inc(s.vc, 1)
-
-    g.sync.wait_ge(s.vc, 2)
-    g.sync.dma_start(T.y[:], T.yo[:]).then_inc(s.st, 16)
+    if is_rank:
+        xa = slice(0, KA)
+        h0, h1 = slice(KA, KA + H), slice(KA + H, W)
+        n_o = n_on * len([f for f in p["folders"] if f != core])
+        n_e = n_off * K
+        t.wait_ge(s.arro, n_o)
+        t.matmul(T.y0[:, 0:H], T.so[:, xa], T.so[:, h0], True, False)
+        t.matmul(T.y1[:, 0:H], T.so[:, xa], T.so[:, h1], True, False)
+        t.wait_ge(s.arre, n_e)
+        t.matmul(T.y0[:, 0:H], T.se[:, xa], T.so[:, h0], False, False)
+        t.matmul(T.y1[:, 0:H], T.se[:, xa], T.so[:, h1], False, False)
+        t.wait_ge(s.va, 1)
+        t.matmul(T.y0[:, 0:H], T.asum[:], T.se[:, h0], False, True).then_inc(s.tm0, 1)
+        t.matmul(T.y1[:, 0:H], T.asum[:], T.se[:, h1], False, True).then_inc(s.tm1, 1)
+        v.wait_ge(s.arro, n_o)
+        v.wait_ge(s.arre, n_e)
+        v.tensor_tensor(T.asum[:], T.so[:, xa], T.se[:, xa], add).then_inc(s.va, 1)
+        v.wait_ge(s.tm0, 1)
+        v.tensor_copy(T.yo[:, 0:H], T.y0[:, 0:H]).then_inc(s.vc, 1)
+        v.wait_ge(s.tm1, 1)
+        v.tensor_copy(T.yo[:, H:F], T.y1[:, 0:H]).then_inc(s.vc, 1)
+        g.sync.wait_ge(s.vc, 2)
+        g.sync.dma_start(T.y[:], T.yo[:]).then_inc(s.st, 16)
 
     g.wait_ge(s.snt, sent)
-    g.wait_ge(s.st, 16)
+    if is_rank:
+        g.wait_ge(s.st, 16)

@@ -4,9 +4,11 @@ from concourse.mybir import AluOpType
 KA = 128
 F = 512
 W = KA + F
-H = F // 2
 K = 4
 PW = W // K
+NW = 2
+PER = K // NW
+PARTS = [(KA, PER * PW, (0, 1)), (2 * PW, 3 * PW, (2,)), (3 * PW, W, (3,))]
 
 SCRATCH = {
     "x": ("sbuf", [128, W], "bfloat16"),
@@ -21,8 +23,11 @@ SCRATCH = {
     "ta": ("psum", [128, 512], "float32"),
     "y0": ("psum", [128, 512], "float32"),
     "y1": ("psum", [128, 512], "float32"),
+    "y2": ("psum", [128, 512], "float32"),
 }
-SEMAPHORES = ["ld", "st", "snt", "arrc", "arrr", "arro", "arre", "sa", "vo", "va", "tm0", "tm1", "vc"]
+SEMAPHORES = (["st", "snt", "arrc", "arrr", "sa", "vo", "va", "ld0", "ld1"]
+              + [n + str(i) for n in ("arro", "arre") for i in range(K)]
+              + [n + str(i) for n in ("tm", "vc") for i in range(len(PARTS))])
 
 
 def _bits(mask):
@@ -48,7 +53,10 @@ def _plan(core, T, topo):
 
     def folders(ch):
         able = [c for c in every if topo.chip(c) == ch and all(topo.may_write(c, d) for d in cores if d != c)]
-        return ([c for c in able if c in cores] + [c for c in able if c not in cores])[:K]
+        last = [c for c in able if c in cores][0]
+        same = [c for c in able if c != last and topo.die(c) == topo.die(last)]
+        away = [c for c in able if topo.die(c) != topo.die(last)]
+        return [away[0], same[0], away[1], last]
 
     mine = sorted([chip] + [ch for ch in chips if topo.same_plane(chip, ch)])
     other = [ch for ch in chips if ch not in mine]
@@ -72,8 +80,9 @@ def rank_program(g, core, T, topo):
     m_off = topo.mask(core, p["far_folders"][0])
     m_on = topo.mask(core, [c for c in p["ranks"] + p["folders"] if c != core][0]) & ~m_off
     n_off, n_on = _bits(m_off), _bits(m_on)
-    g_off, g_on = _groups(m_off, K), _groups(m_on, K)
+    g_off, g_on = _groups(m_off, PER), _groups(m_on, PER)
     cs = [slice(i * PW, (i + 1) * PW) for i in range(K)]
+    n_ld = (32, 16)
     v, t = g.vector, g.tensor
     sent = 0
 
@@ -82,72 +91,83 @@ def rank_program(g, core, T, topo):
         return DstId(rid=rid, pnc=pid)
 
     if is_rank:
-        g.sync.dma_start(T.x[:, 0:KA], T.a[:]).then_inc(s.ld, 16)
-        g.scalar.dma_start(T.x[:, KA:W], T.b[:]).then_inc(s.ld, 16)
-        g.wait_ge(s.ld, 32)
+        cut = PER * PW
+        g.sync.dma_start(T.x[:, 0:KA], T.a[:]).then_inc(s.ld0, 16)
+        g.scalar.dma_start(T.x[:, KA:cut], T.b[:, 0:cut - KA]).then_inc(s.ld0, 16)
+        g.sync.dma_start(T.x[:, cut:W], T.b[:, cut - KA:F]).then_inc(s.ld1, 16)
         me = p["ranks"].index(core)
         far, near = (T.lr0, T.lr1)[me], (T.lc0, T.lc1)[me]
-        g.remote_dma_fused([RemoteDMATransfer(dst_ids=[dst(f)], dma_engine_mask=g_off[i], remote_sem=s.arrr,
-                                              src=T.x[:, cs[i]], dst=far[:, cs[i]])
-                            for i, f in enumerate(p["far_folders"])], local_sem=s.snt)
-        g.remote_dma_fused([RemoteDMATransfer(dst_ids=[dst(f)], dma_engine_mask=g_on[i], remote_sem=s.arrc,
-                                              src=T.x[:, cs[i]], dst=near[:, cs[i]])
-                            for i, f in enumerate(p["folders"]) if f != core], local_sem=s.snt)
-        sent += n_off + sum(_bits(g_on[i]) for i, f in enumerate(p["folders"]) if f != core)
+        for w in range(NW):
+            g.wait_ge(s["ld%d" % w], n_ld[w])
+            tr = []
+            for h in range(PER):
+                i = w * PER + h
+                tr.append(RemoteDMATransfer(dst_ids=[dst(p["far_folders"][i])], dma_engine_mask=g_off[h],
+                                            remote_sem=s.arrr, src=T.x[:, cs[i]], dst=far[:, cs[i]]))
+                sent += _bits(g_off[h])
+                if p["folders"][i] != core:
+                    tr.append(RemoteDMATransfer(dst_ids=[dst(p["folders"][i])], dma_engine_mask=g_on[h],
+                                                remote_sem=s.arrc, src=T.x[:, cs[i]], dst=near[:, cs[i]]))
+                    sent += _bits(g_on[h])
+            g.remote_dma_fused(tr, local_sem=s.snt)
 
     if is_folder:
         j = p["folders"].index(core)
         c = cs[j]
-        n_c = _bits(g_on[j]) * len([r for r in p["ranks"] if r != core])
-        n_r = _bits(g_off[j]) * len(p["ranks"])
-        here = [T.x if r == core else (T.lc0, T.lc1)[i] for i, r in enumerate(p["ranks"])]
-        four = here + [T.lr0, T.lr1]
         home = [r for r in p["ranks"] if r != core]
+        n_c = _bits(g_on[j % PER]) * len(home)
+        n_r = _bits(g_off[j % PER]) * len(p["ranks"])
+        four = [T.x if r == core else (T.lc0, T.lc1)[i] for i, r in enumerate(p["ranks"])] + [T.lr0, T.lr1]
         g.wait_ge(s.arrc, n_c)
         g.wait_ge(s.arrr, n_r)
         g.remote_dma_fused([RemoteDMATransfer(dst_ids=[dst(r) for r in p["across"]], dma_engine_mask=m_off,
-                                              remote_sem=s.arre, srcs=[q[:, c] for q in four],
+                                              remote_sem=s["arre%d" % j], srcs=[q[:, c] for q in four],
                                               dsts=[T.se[:, c] for _ in p["across"]], alu_op=1),
                             RemoteDMATransfer(dst_ids=[dst(r) for r in home], dma_engine_mask=m_on,
-                                              remote_sem=s.arro, srcs=[q[:, c] for q in four],
+                                              remote_sem=s["arro%d" % j], srcs=[q[:, c] for q in four],
                                               dsts=[T.so[:, c] for _ in home], alu_op=1)], local_sem=s.snt)
         sent += n_off + n_on
         if is_rank:
-            v.wait_ge(s.ld, 32)
+            acc = T.ta[:, 0:PW]
+            v.wait_ge(s["ld%d" % (j // PER)], n_ld[j // PER])
             v.wait_ge(s.arrc, n_c)
-            v.tensor_tensor(T.ta[:, 0:PW], four[0][:, c], four[1][:, c], add).then_inc(s.sa, 1)
+            v.tensor_tensor(acc, four[0][:, c], four[1][:, c], add).then_inc(s.sa, 1)
             v.wait_ge(s.arrr, n_r)
             v.wait_ge(s.sa, 1)
-            v.tensor_tensor(T.ta[:, 0:PW], T.ta[:, 0:PW], four[2][:, c], add).then_inc(s.sa, 1)
+            v.tensor_tensor(acc, acc, four[2][:, c], add).then_inc(s.sa, 1)
             v.wait_ge(s.sa, 2)
-            v.tensor_tensor(T.so[:, c], T.ta[:, 0:PW], four[3][:, c], add).then_inc(s.vo, 1)
-            v.wait_ge(s.vo, 1)
-            t.wait_ge(s.vo, 1)
+            v.tensor_tensor(T.so[:, c], acc, four[3][:, c], add).then_inc(s.vo, 1)
 
     if is_rank:
-        xa = slice(0, KA)
-        h0, h1 = slice(KA, KA + H), slice(KA + H, W)
-        n_o = n_on * len([f for f in p["folders"] if f != core])
-        n_e = n_off * K
-        t.wait_ge(s.arro, n_o)
-        t.matmul(T.y0[:, 0:H], T.so[:, xa], T.so[:, h0], True, False)
-        t.matmul(T.y1[:, 0:H], T.so[:, xa], T.so[:, h1], True, False)
-        t.wait_ge(s.arre, n_e)
-        t.matmul(T.y0[:, 0:H], T.se[:, xa], T.so[:, h0], False, False)
-        t.matmul(T.y1[:, 0:H], T.se[:, xa], T.so[:, h1], False, False)
+        def wait_o(q, i):
+            if p["folders"][i] == core:
+                q.wait_ge(s.vo, 1)
+            else:
+                q.wait_ge(s["arro%d" % i], n_on)
+
+        wait_o(v, 0)
+        v.wait_ge(s.arre0, n_off)
+        v.tensor_tensor(T.asum[:], T.so[:, 0:KA], T.se[:, 0:KA], add).then_inc(s.va, 1)
         t.wait_ge(s.va, 1)
-        t.matmul(T.y0[:, 0:H], T.asum[:], T.se[:, h0], False, True).then_inc(s.tm0, 1)
-        t.matmul(T.y1[:, 0:H], T.asum[:], T.se[:, h1], False, True).then_inc(s.tm1, 1)
-        v.wait_ge(s.arro, n_o)
-        v.wait_ge(s.arre, n_e)
-        v.tensor_tensor(T.asum[:], T.so[:, xa], T.se[:, xa], add).then_inc(s.va, 1)
-        v.wait_ge(s.tm0, 1)
-        v.tensor_copy(T.yo[:, 0:H], T.y0[:, 0:H]).then_inc(s.vc, 1)
-        v.wait_ge(s.tm1, 1)
-        v.tensor_copy(T.yo[:, H:F], T.y1[:, 0:H]).then_inc(s.vc, 1)
-        g.sync.wait_ge(s.vc, 2)
-        g.sync.dma_start(T.y[:], T.yo[:]).then_inc(s.st, 16)
+        order = [(0, "o"), (0, "e"), (1, "o"), (2, "o"), (1, "e"), (2, "e")]
+        for k, side in order:
+            lo, hi, blocks = PARTS[k]
+            yp = T["y%d" % k][:, 0:hi - lo]
+            if side == "o":
+                for i in blocks:
+                    wait_o(t, i)
+                t.matmul(yp, T.asum[:], T.so[:, lo:hi], True, False)
+            else:
+                for i in blocks:
+                    t.wait_ge(s["arre%d" % i], n_off)
+                t.matmul(yp, T.asum[:], T.se[:, lo:hi], False, True).then_inc(s["tm%d" % k], 1)
+        for k, q in enumerate((g.scalar, g.sync, g.scalar)):
+            lo, hi, _ = PARTS[k]
+            v.wait_ge(s["tm%d" % k], 1)
+            v.tensor_copy(T.yo[:, lo - KA:hi - KA], T["y%d" % k][:, 0:hi - lo]).then_inc(s["vc%d" % k], 1)
+            q.wait_ge(s["vc%d" % k], 1)
+            q.dma_start(T.y[:, lo - KA:hi - KA], T.yo[:, lo - KA:hi - KA]).then_inc(s.st, 16)
 
     g.wait_ge(s.snt, sent)
     if is_rank:
-        g.wait_ge(s.st, 16)
+        g.wait_ge(s.st, 16 * len(PARTS))

@@ -3,21 +3,35 @@ from concourse.mybir import AluOpType
 
 KA = 128
 F = 512
-W = KA + F
 K = 4
-PW = W // K
+PW = F // K
 NW = 2
 PER = K // NW
-PARTS = [(KA, PER * PW, (0, 1)), (2 * PW, 3 * PW, (2,)), (3 * PW, W, (3,))]
+CW = KA // K
+PARTS = [(0, PER * PW, (0, 1)), (2 * PW, 3 * PW, (2,)), (3 * PW, F, (3,))]
 
 SCRATCH = {
-    "x": ("sbuf", [128, W], "bfloat16"),
-    "lc0": ("sbuf", [128, W], "bfloat16"),
-    "lc1": ("sbuf", [128, W], "bfloat16"),
-    "lr0": ("sbuf", [128, W], "bfloat16"),
-    "lr1": ("sbuf", [128, W], "bfloat16"),
-    "so": ("sbuf", [128, W], "bfloat16"),
-    "se": ("sbuf", [128, W], "bfloat16"),
+    "x": ("sbuf", [128, F], "bfloat16"),
+    "lc0": ("sbuf", [128, F], "bfloat16"),
+    "lc1": ("sbuf", [128, F], "bfloat16"),
+    "lr0": ("sbuf", [128, F], "bfloat16"),
+    "lr1": ("sbuf", [128, F], "bfloat16"),
+    "xd": ("dram", [K * 128, PW], "bfloat16"),
+    "dc0": ("dram", [128, PW], "bfloat16"),
+    "dc1": ("dram", [128, PW], "bfloat16"),
+    "dr0": ("dram", [128, PW], "bfloat16"),
+    "dr1": ("dram", [128, PW], "bfloat16"),
+    "so": ("sbuf", [128, F], "bfloat16"),
+    "se": ("sbuf", [128, F], "bfloat16"),
+    "ad": ("dram", [K * 128, CW], "bfloat16"),
+    "ac0": ("dram", [K * 128, CW], "bfloat16"),
+    "ac1": ("dram", [K * 128, CW], "bfloat16"),
+    "ar0": ("dram", [K * 128, CW], "bfloat16"),
+    "ar1": ("dram", [K * 128, CW], "bfloat16"),
+    "ao": ("dram", [K * 128, CW], "bfloat16"),
+    "ae": ("dram", [K * 128, CW], "bfloat16"),
+    "oa": ("sbuf", [128, KA], "bfloat16"),
+    "ea": ("sbuf", [128, KA], "bfloat16"),
     "asum": ("sbuf", [128, KA], "bfloat16"),
     "yo": ("sbuf", [128, F], "bfloat16"),
     "ta": ("psum", [128, 512], "float32"),
@@ -25,7 +39,7 @@ SCRATCH = {
     "y1": ("psum", [128, 512], "float32"),
     "y2": ("psum", [128, 512], "float32"),
 }
-SEMAPHORES = (["st", "snt", "arrc", "arrr", "sa", "vo", "va", "ld0", "ld1"]
+SEMAPHORES = (["st", "snt", "arrc", "arrr", "sa", "vo", "va", "lda", "ld0", "ld1", "aarr", "arrao", "arrae", "la"]
               + [n + str(i) for n in ("arro", "arre") for i in range(K)]
               + [n + str(i) for n in ("tm", "vc") for i in range(len(PARTS))])
 
@@ -69,6 +83,10 @@ def _plan(core, T, topo):
     }
 
 
+def _owners(f):
+    return [f[0], f[1], f[2], f[1]]
+
+
 def rank_program(g, core, T, topo):
     p = _plan(core, T, topo)
     if p is None or (core not in p["ranks"] and core not in p["folders"]):
@@ -81,8 +99,12 @@ def rank_program(g, core, T, topo):
     m_on = topo.mask(core, [c for c in p["ranks"] + p["folders"] if c != core][0]) & ~m_off
     n_off, n_on = _bits(m_off), _bits(m_on)
     g_off, g_on = _groups(m_off, PER), _groups(m_on, PER)
+    a_off, a_on = _groups(m_off, K), _groups(m_on, K)
     cs = [slice(i * PW, (i + 1) * PW) for i in range(K)]
-    n_ld = (32, 16)
+    ck = [slice(k * 128, (k + 1) * 128) for k in range(K)]
+    own, far_own = _owners(p["folders"]), _owners(p["far_folders"])
+    flat = [f not in p["ranks"] for f in p["folders"]]
+    n_ld = 16 * PER
     v, t = g.vector, g.tensor
     sent = 0
 
@@ -91,25 +113,54 @@ def rank_program(g, core, T, topo):
         return DstId(rid=rid, pnc=pid)
 
     if is_rank:
-        cut = PER * PW
-        g.sync.dma_start(T.x[:, 0:KA], T.a[:]).then_inc(s.ld0, 16)
-        g.scalar.dma_start(T.x[:, KA:cut], T.b[:, 0:cut - KA]).then_inc(s.ld0, 16)
-        g.sync.dma_start(T.x[:, cut:W], T.b[:, cut - KA:F]).then_inc(s.ld1, 16)
+        g.sync.dma_start(T.ad[:], T.a[:]).then_inc(s.lda, 16)
+        for i in range(K):
+            q = (g.scalar, g.sync)[i % PER]
+            q.dma_start(T.xd[ck[i], :] if flat[i] else T.x[:, cs[i]], T.b[:, cs[i]]).then_inc(s["ld%d" % (i // PER)], 16)
         me = p["ranks"].index(core)
-        far, near = (T.lr0, T.lr1)[me], (T.lc0, T.lc1)[me]
+        afar, anear = (T.ar0, T.ar1)[me], (T.ac0, T.ac1)[me]
+        g.wait_ge(s.lda, 16)
+        tr = []
+        for k in range(K):
+            tr.append(RemoteDMATransfer(dst_ids=[dst(far_own[k])], dma_engine_mask=a_off[k], remote_sem=s.aarr,
+                                        src=T.ad[ck[k], :], dst=afar[ck[k], :]))
+            tr.append(RemoteDMATransfer(dst_ids=[dst(own[k])], dma_engine_mask=a_on[k], remote_sem=s.aarr,
+                                        src=T.ad[ck[k], :], dst=anear[ck[k], :]))
+            sent += _bits(a_off[k]) + _bits(a_on[k])
+        g.remote_dma_fused(tr, local_sem=s.snt)
         for w in range(NW):
-            g.wait_ge(s["ld%d" % w], n_ld[w])
+            g.wait_ge(s["ld%d" % w], n_ld)
             tr = []
             for h in range(PER):
                 i = w * PER + h
+                if flat[i]:
+                    src, far, near = T.xd[ck[i], :], (T.dr0, T.dr1)[me][:], (T.dc0, T.dc1)[me][:]
+                else:
+                    src, far, near = T.x[:, cs[i]], (T.lr0, T.lr1)[me][:, cs[i]], (T.lc0, T.lc1)[me][:, cs[i]]
                 tr.append(RemoteDMATransfer(dst_ids=[dst(p["far_folders"][i])], dma_engine_mask=g_off[h],
-                                            remote_sem=s.arrr, src=T.x[:, cs[i]], dst=far[:, cs[i]]))
+                                            remote_sem=s.arrr, src=src, dst=far))
                 sent += _bits(g_off[h])
                 if p["folders"][i] != core:
                     tr.append(RemoteDMATransfer(dst_ids=[dst(p["folders"][i])], dma_engine_mask=g_on[h],
-                                                remote_sem=s.arrc, src=T.x[:, cs[i]], dst=near[:, cs[i]]))
+                                                remote_sem=s.arrc, src=src, dst=near))
                     sent += _bits(g_on[h])
             g.remote_dma_fused(tr, local_sem=s.snt)
+
+    mine_k = [k for k in range(K) if own[k] == core]
+    if mine_k:
+        g.wait_ge(s.aarr, sum(_bits(a_off[k]) + _bits(a_on[k]) for k in mine_k) * len(p["ranks"]))
+        h_off, h_on = _groups(m_off, len(mine_k)), _groups(m_on, len(mine_k))
+        tr = []
+        for n, k in enumerate(mine_k):
+            four = [q[ck[k], :] for q in (T.ac0, T.ac1, T.ar0, T.ar1)]
+            tr.append(RemoteDMATransfer(dst_ids=[dst(r) for r in p["across"]], dma_engine_mask=h_off[n],
+                                        remote_sem=s.arrae, srcs=four,
+                                        dsts=[T.ae[ck[k], :] for _ in p["across"]], alu_op=1))
+            tr.append(RemoteDMATransfer(dst_ids=[dst(r) for r in p["ranks"]], dma_engine_mask=h_on[n],
+                                        remote_sem=s.arrao, srcs=four,
+                                        dsts=[T.ao[ck[k], :] for _ in p["ranks"]], alu_op=1))
+            sent += _bits(h_off[n]) + _bits(h_on[n])
+        g.remote_dma_fused(tr, local_sem=s.snt)
 
     if is_folder:
         j = p["folders"].index(core)
@@ -117,26 +168,30 @@ def rank_program(g, core, T, topo):
         home = [r for r in p["ranks"] if r != core]
         n_c = _bits(g_on[j % PER]) * len(home)
         n_r = _bits(g_off[j % PER]) * len(p["ranks"])
-        four = [T.x if r == core else (T.lc0, T.lc1)[i] for i, r in enumerate(p["ranks"])] + [T.lr0, T.lr1]
+        if flat[j]:
+            four = [q[:] for q in (T.dc0, T.dc1, T.dr0, T.dr1)]
+        else:
+            four = [q[:, c] for q in [T.x if r == core else (T.lc0, T.lc1)[i] for i, r in enumerate(p["ranks"])]
+                    + [T.lr0, T.lr1]]
         g.wait_ge(s.arrc, n_c)
         g.wait_ge(s.arrr, n_r)
         g.remote_dma_fused([RemoteDMATransfer(dst_ids=[dst(r) for r in p["across"]], dma_engine_mask=m_off,
-                                              remote_sem=s["arre%d" % j], srcs=[q[:, c] for q in four],
+                                              remote_sem=s["arre%d" % j], srcs=four,
                                               dsts=[T.se[:, c] for _ in p["across"]], alu_op=1),
                             RemoteDMATransfer(dst_ids=[dst(r) for r in home], dma_engine_mask=m_on,
-                                              remote_sem=s["arro%d" % j], srcs=[q[:, c] for q in four],
+                                              remote_sem=s["arro%d" % j], srcs=four,
                                               dsts=[T.so[:, c] for _ in home], alu_op=1)], local_sem=s.snt)
         sent += n_off + n_on
         if is_rank:
             acc = T.ta[:, 0:PW]
-            v.wait_ge(s["ld%d" % (j // PER)], n_ld[j // PER])
+            v.wait_ge(s["ld%d" % (j // PER)], n_ld)
             v.wait_ge(s.arrc, n_c)
-            v.tensor_tensor(acc, four[0][:, c], four[1][:, c], add).then_inc(s.sa, 1)
+            v.tensor_tensor(acc, four[0], four[1], add).then_inc(s.sa, 1)
             v.wait_ge(s.arrr, n_r)
             v.wait_ge(s.sa, 1)
-            v.tensor_tensor(acc, acc, four[2][:, c], add).then_inc(s.sa, 1)
+            v.tensor_tensor(acc, acc, four[2], add).then_inc(s.sa, 1)
             v.wait_ge(s.sa, 2)
-            v.tensor_tensor(T.so[:, c], acc, four[3][:, c], add).then_inc(s.vo, 1)
+            v.tensor_tensor(T.so[:, c], acc, four[3], add).then_inc(s.vo, 1)
 
     if is_rank:
         def wait_o(q, i):
@@ -145,9 +200,13 @@ def rank_program(g, core, T, topo):
             else:
                 q.wait_ge(s["arro%d" % i], n_on)
 
-        wait_o(v, 0)
-        v.wait_ge(s.arre0, n_off)
-        v.tensor_tensor(T.asum[:], T.so[:, 0:KA], T.se[:, 0:KA], add).then_inc(s.va, 1)
+        helpers = sorted(set(own))
+        g.sync.wait_ge(s.arrao, n_on * len(helpers))
+        g.sync.dma_start(T.oa[:], T.ao[:]).then_inc(s.la, 16)
+        g.scalar.wait_ge(s.arrae, n_off * len(helpers))
+        g.scalar.dma_start(T.ea[:], T.ae[:]).then_inc(s.la, 16)
+        v.wait_ge(s.la, 32)
+        v.tensor_tensor(T.asum[:], T.oa[:], T.ea[:], add).then_inc(s.va, 1)
         t.wait_ge(s.va, 1)
         order = [(0, "o"), (0, "e"), (1, "o"), (2, "o"), (1, "e"), (2, "e")]
         for k, side in order:
@@ -164,9 +223,9 @@ def rank_program(g, core, T, topo):
         for k, q in enumerate((g.scalar, g.sync, g.scalar)):
             lo, hi, _ = PARTS[k]
             v.wait_ge(s["tm%d" % k], 1)
-            v.tensor_copy(T.yo[:, lo - KA:hi - KA], T["y%d" % k][:, 0:hi - lo]).then_inc(s["vc%d" % k], 1)
+            v.tensor_copy(T.yo[:, lo:hi], T["y%d" % k][:, 0:hi - lo]).then_inc(s["vc%d" % k], 1)
             q.wait_ge(s["vc%d" % k], 1)
-            q.dma_start(T.y[:, lo - KA:hi - KA], T.yo[:, lo - KA:hi - KA]).then_inc(s.st, 16)
+            q.dma_start(T.y[:, lo:hi], T.yo[:, lo:hi]).then_inc(s.st, 16)
 
     g.wait_ge(s.snt, sent)
     if is_rank:

from concourse.bass import DstId, RemoteDMATransfer
from concourse.mybir import AluOpType

KA = 128
F = 512
K = 4
PW = F // K
NW = 2
PER = K // NW
CW = KA // K
PARTS = [(0, PER * PW, (0, 1)), (2 * PW, 3 * PW, (2,)), (3 * PW, F, (3,))]

SCRATCH = {
    "x": ("sbuf", [128, F], "bfloat16"),
    "lc0": ("sbuf", [128, F], "bfloat16"),
    "lc1": ("sbuf", [128, F], "bfloat16"),
    "lr0": ("sbuf", [128, F], "bfloat16"),
    "lr1": ("sbuf", [128, F], "bfloat16"),
    "xd": ("dram", [K * 128, PW], "bfloat16"),
    "dc0": ("dram", [128, PW], "bfloat16"),
    "dc1": ("dram", [128, PW], "bfloat16"),
    "dr0": ("dram", [128, PW], "bfloat16"),
    "dr1": ("dram", [128, PW], "bfloat16"),
    "so": ("sbuf", [128, F], "bfloat16"),
    "se": ("sbuf", [128, F], "bfloat16"),
    "ad": ("dram", [K * 128, CW], "bfloat16"),
    "ac0": ("dram", [K * 128, CW], "bfloat16"),
    "ac1": ("dram", [K * 128, CW], "bfloat16"),
    "ar0": ("dram", [K * 128, CW], "bfloat16"),
    "ar1": ("dram", [K * 128, CW], "bfloat16"),
    "ao": ("dram", [K * 128, CW], "bfloat16"),
    "ae": ("dram", [K * 128, CW], "bfloat16"),
    "oa": ("sbuf", [128, KA], "bfloat16"),
    "ea": ("sbuf", [128, KA], "bfloat16"),
    "asum": ("sbuf", [128, KA], "bfloat16"),
    "yo": ("sbuf", [128, F], "bfloat16"),
    "ta": ("psum", [128, 512], "float32"),
    "y0": ("psum", [128, 512], "float32"),
    "y1": ("psum", [128, 512], "float32"),
    "y2": ("psum", [128, 512], "float32"),
}
SEMAPHORES = (["st", "snt", "arrc", "arrr", "sa", "vo", "va", "lda", "ld0", "ld1", "aarr", "arrao", "arrae", "la"]
              + [n + str(i) for n in ("arro", "arre") for i in range(K)]
              + [n + str(i) for n in ("tm", "vc") for i in range(len(PARTS))])


def _bits(mask):
    return bin(mask).count("1")


def _groups(mask, k):
    b = [1 << i for i in range(mask.bit_length()) if mask >> i & 1]
    n = len(b) // k
    return [sum(b[i * n:(i + 1) * n]) for i in range(k)]


def _plan(core, T, topo):
    cores = list(T.cores)
    chip = topo.chip(core)
    chips = sorted({topo.chip(c) for c in cores})
    if chip not in chips:
        return None
    every = range(topo.CHIPS * topo.CORES_PER_CHIP)

    def ranks(ch):
        return [c for c in cores if topo.chip(c) == ch]

    def folders(ch):
        able = [c for c in every if topo.chip(c) == ch and all(topo.may_write(c, d) for d in cores if d != c)]
        last = [c for c in able if c in cores][0]
        same = [c for c in able if c != last and topo.die(c) == topo.die(last)]
        away = [c for c in able if topo.die(c) != topo.die(last)]
        return [away[0], same[0], away[1], last]

    mine = sorted([chip] + [ch for ch in chips if topo.same_plane(chip, ch)])
    other = [ch for ch in chips if ch not in mine]
    partner = [ch for ch in mine if ch != chip][0]
    return {
        "ranks": ranks(chip),
        "folders": folders(chip),
        "far_folders": folders(partner),
        "across": ranks(other[mine.index(chip)]),
    }


def _owners(f):
    return [f[0], f[1], f[2], f[1]]


def rank_program(g, core, T, topo):
    p = _plan(core, T, topo)
    if p is None or (core not in p["ranks"] and core not in p["folders"]):
        return
    s = T.sem
    add = AluOpType.add
    is_rank = core in p["ranks"]
    is_folder = core in p["folders"]
    m_off = topo.mask(core, p["far_folders"][0])
    m_on = topo.mask(core, [c for c in p["ranks"] + p["folders"] if c != core][0]) & ~m_off
    n_off, n_on = _bits(m_off), _bits(m_on)
    g_off, g_on = _groups(m_off, PER), _groups(m_on, PER)
    a_off, a_on = _groups(m_off, K), _groups(m_on, K)
    cs = [slice(i * PW, (i + 1) * PW) for i in range(K)]
    ck = [slice(k * 128, (k + 1) * 128) for k in range(K)]
    own, far_own = _owners(p["folders"]), _owners(p["far_folders"])
    flat = [f not in p["ranks"] for f in p["folders"]]
    n_ld = 16 * PER
    v, t = g.vector, g.tensor
    sent = 0

    def dst(c):
        rid, pid, _ = topo.addr(c)
        return DstId(rid=rid, pnc=pid)

    if is_rank:
        g.sync.dma_start(T.ad[:], T.a[:]).then_inc(s.lda, 16)
        for i in range(K):
            q = (g.scalar, g.sync)[i % PER]
            q.dma_start(T.xd[ck[i], :] if flat[i] else T.x[:, cs[i]], T.b[:, cs[i]]).then_inc(s["ld%d" % (i // PER)], 16)
        me = p["ranks"].index(core)
        afar, anear = (T.ar0, T.ar1)[me], (T.ac0, T.ac1)[me]
        g.wait_ge(s.lda, 16)
        tr = []
        for k in range(K):
            tr.append(RemoteDMATransfer(dst_ids=[dst(far_own[k])], dma_engine_mask=a_off[k], remote_sem=s.aarr,
                                        src=T.ad[ck[k], :], dst=afar[ck[k], :]))
            tr.append(RemoteDMATransfer(dst_ids=[dst(own[k])], dma_engine_mask=a_on[k], remote_sem=s.aarr,
                                        src=T.ad[ck[k], :], dst=anear[ck[k], :]))
            sent += _bits(a_off[k]) + _bits(a_on[k])
        g.remote_dma_fused(tr, local_sem=s.snt)
        for w in range(NW):
            g.wait_ge(s["ld%d" % w], n_ld)
            tr = []
            for h in range(PER):
                i = w * PER + h
                if flat[i]:
                    src, far, near = T.xd[ck[i], :], (T.dr0, T.dr1)[me][:], (T.dc0, T.dc1)[me][:]
                else:
                    src, far, near = T.x[:, cs[i]], (T.lr0, T.lr1)[me][:, cs[i]], (T.lc0, T.lc1)[me][:, cs[i]]
                tr.append(RemoteDMATransfer(dst_ids=[dst(p["far_folders"][i])], dma_engine_mask=g_off[h],
                                            remote_sem=s.arrr, src=src, dst=far))
                sent += _bits(g_off[h])
                if p["folders"][i] != core:
                    tr.append(RemoteDMATransfer(dst_ids=[dst(p["folders"][i])], dma_engine_mask=g_on[h],
                                                remote_sem=s.arrc, src=src, dst=near))
                    sent += _bits(g_on[h])
            g.remote_dma_fused(tr, local_sem=s.snt)

    mine_k = [k for k in range(K) if own[k] == core]
    if mine_k:
        g.wait_ge(s.aarr, sum(_bits(a_off[k]) + _bits(a_on[k]) for k in mine_k) * len(p["ranks"]))
        h_off, h_on = _groups(m_off, len(mine_k)), _groups(m_on, len(mine_k))
        tr = []
        for n, k in enumerate(mine_k):
            four = [q[ck[k], :] for q in (T.ac0, T.ac1, T.ar0, T.ar1)]
            tr.append(RemoteDMATransfer(dst_ids=[dst(r) for r in p["across"]], dma_engine_mask=h_off[n],
                                        remote_sem=s.arrae, srcs=four,
                                        dsts=[T.ae[ck[k], :] for _ in p["across"]], alu_op=1))
            tr.append(RemoteDMATransfer(dst_ids=[dst(r) for r in p["ranks"]], dma_engine_mask=h_on[n],
                                        remote_sem=s.arrao, srcs=four,
                                        dsts=[T.ao[ck[k], :] for _ in p["ranks"]], alu_op=1))
            sent += _bits(h_off[n]) + _bits(h_on[n])
        g.remote_dma_fused(tr, local_sem=s.snt)

    if is_folder:
        j = p["folders"].index(core)
        c = cs[j]
        home = [r for r in p["ranks"] if r != core]
        n_c = _bits(g_on[j % PER]) * len(home)
        n_r = _bits(g_off[j % PER]) * len(p["ranks"])
        if flat[j]:
            four = [q[:] for q in (T.dc0, T.dc1, T.dr0, T.dr1)]
        else:
            four = [q[:, c] for q in [T.x if r == core else (T.lc0, T.lc1)[i] for i, r in enumerate(p["ranks"])]
                    + [T.lr0, T.lr1]]
        g.wait_ge(s.arrc, n_c)
        g.wait_ge(s.arrr, n_r)
        g.remote_dma_fused([RemoteDMATransfer(dst_ids=[dst(r) for r in p["across"]], dma_engine_mask=m_off,
                                              remote_sem=s["arre%d" % j], srcs=four,
                                              dsts=[T.se[:, c] for _ in p["across"]], alu_op=1),
                            RemoteDMATransfer(dst_ids=[dst(r) for r in home], dma_engine_mask=m_on,
                                              remote_sem=s["arro%d" % j], srcs=four,
                                              dsts=[T.so[:, c] for _ in home], alu_op=1)], local_sem=s.snt)
        sent += n_off + n_on
        if is_rank:
            acc = T.ta[:, 0:PW]
            v.wait_ge(s["ld%d" % (j // PER)], n_ld)
            v.wait_ge(s.arrc, n_c)
            v.tensor_tensor(acc, four[0], four[1], add).then_inc(s.sa, 1)
            v.wait_ge(s.arrr, n_r)
            v.wait_ge(s.sa, 1)
            v.tensor_tensor(acc, acc, four[2], add).then_inc(s.sa, 1)
            v.wait_ge(s.sa, 2)
            v.tensor_tensor(T.so[:, c], acc, four[3], add).then_inc(s.vo, 1)

    if is_rank:
        def wait_o(q, i):
            if p["folders"][i] == core:
                q.wait_ge(s.vo, 1)
            else:
                q.wait_ge(s["arro%d" % i], n_on)

        helpers = sorted(set(own))
        g.sync.wait_ge(s.arrao, n_on * len(helpers))
        g.sync.dma_start(T.oa[:], T.ao[:]).then_inc(s.la, 16)
        g.scalar.wait_ge(s.arrae, n_off * len(helpers))
        g.scalar.dma_start(T.ea[:], T.ae[:]).then_inc(s.la, 16)
        v.wait_ge(s.la, 32)
        v.tensor_tensor(T.asum[:], T.oa[:], T.ea[:], add).then_inc(s.va, 1)
        t.wait_ge(s.va, 1)
        order = [(0, "o"), (0, "e"), (1, "o"), (2, "o"), (1, "e"), (2, "e")]
        for k, side in order:
            lo, hi, blocks = PARTS[k]
            yp = T["y%d" % k][:, 0:hi - lo]
            if side == "o":
                for i in blocks:
                    wait_o(t, i)
                t.matmul(yp, T.asum[:], T.so[:, lo:hi], True, False)
            else:
                for i in blocks:
                    t.wait_ge(s["arre%d" % i], n_off)
                t.matmul(yp, T.asum[:], T.se[:, lo:hi], False, True).then_inc(s["tm%d" % k], 1)
        for k, q in enumerate((g.scalar, g.sync, g.scalar)):
            lo, hi, _ = PARTS[k]
            v.wait_ge(s["tm%d" % k], 1)
            v.tensor_copy(T.yo[:, lo:hi], T["y%d" % k][:, 0:hi - lo]).then_inc(s["vc%d" % k], 1)
            q.wait_ge(s["vc%d" % k], 1)
            q.dma_start(T.y[:, lo:hi], T.yo[:, lo:hi]).then_inc(s.st, 16)

    g.wait_ge(s.snt, sent)
    if is_rank:
        g.wait_ge(s.st, 16 * len(PARTS))
